import numpy as np
import ml_dtypes


def mxq(x, axis, fmt="e4m3"):
    dtype, down = {"e4m3": (ml_dtypes.float8_e4m3fn, 7), "e5m2": (ml_dtypes.float8_e5m2, 14)}[fmt]
    v = np.moveaxis(np.asarray(x, np.float32).astype(ml_dtypes.bfloat16).astype(np.float64), axis, -1)
    blocks = v.reshape(v.shape[:-1] + (-1, 32))
    amax = np.abs(blocks).max(-1, keepdims=True)
    byte = np.maximum(np.where(amax > 0, np.frexp(amax)[1] - 1 + 127, 0) - down, 1)
    scale = np.exp2(byte - 127.0)
    codes = (blocks / scale).astype(np.float32).astype(dtype).astype(np.float64)
    return np.moveaxis((codes * scale).reshape(v.shape), -1, axis)


WIDE = False


def mx_kscale(k):
    if not WIDE:
        return np.ones(k)
    levels = np.array([10, -10, 5, -5, 0])
    if k % 512:
        return np.exp2(np.random.permutation(np.resize(levels, k // 32))).repeat(32)
    a = np.empty((k // 512, 16))
    for p in range(k // 512):
        a[p, :8] = np.random.permutation(np.resize(levels, 8))
        for g in range(8):
            far = levels[np.abs(levels - a[p, g]) >= 10]
            a[p, g + 8] = far[np.random.randint(len(far))]
    return np.exp2(a.ravel()).repeat(32)


def f64(x):
    return np.asarray(x).astype(np.float64)


def striped(idx):
    return np.tile(idx.reshape(-1, 16).T, (8, 1)).astype(np.uint16)


def unstriped(offs):
    return offs[:16].T.reshape(-1).astype(np.int64)


def pack_weight(w):
    k, n = w.shape
    w = f64(np.asarray(w, np.float32).astype(ml_dtypes.bfloat16)).reshape(k // 32, 32, n)
    amax = np.abs(w).max(1)
    byte = np.clip(np.where(amax > 0, np.frexp(amax)[1] - 1 + 127 - 7, 1), 1, 254)
    scaled = (w * np.exp2(127.0 - byte)[:, None, :]).reshape(k, n).astype(np.float32)
    words = np.ascontiguousarray(scaled.reshape(k // 512, 128, 4, n).transpose(0, 1, 3, 2)).astype(ml_dtypes.float8_e4m3fn).view(np.uint8)
    return words, np.ascontiguousarray(byte.astype(np.uint8).reshape(k // 512, 16, n))


def unpack_weight(words, scales):
    g, p, n, _ = words.shape
    vals = np.ascontiguousarray(words).view(ml_dtypes.float8_e4m3fn).astype(np.float64) * np.repeat(np.exp2(scales.astype(np.float64) - 127.0), 8, axis=1)[..., None]
    return vals.transpose(0, 1, 3, 2).reshape(g * 512, n)


def sigmoid(v):
    return 1.0 / (1.0 + np.exp(-np.maximum(v, -700.0)))


K, T, S, H, W, C = 512, 2048, 512, 512, 256, 512


def setup_inputs():
    n = np.random.standard_normal
    s = mx_kscale(K)[:, None]
    packed_xT = pack_weight(n((K, T)) * s)
    perm = np.random.permutation(S)
    return {
        "x_words": packed_xT[0],
        "x_scales": packed_xT[1],
        "w1": (n((K, H)) / np.sqrt(K) / s).astype(np.float32),
        "gs": (np.random.uniform(0.5, 1.5, (K, 1)) / s).astype(np.float32),
        "wb": (n((K, S)) / np.sqrt(K) / s).astype(np.float32),
        "offs": striped(np.random.permutation(T)[:S]),
        "n1": striped(perm[:W]),
        "n2": striped(perm[W:]),
        "cand": striped(np.random.permutation(T)[:C]),
        "cb": striped(np.random.permutation(T)[:C]),
        "n3": striped(np.random.permutation(S)),
        "n4": striped(np.random.permutation(S)),
    }


def reference(x_words, x_scales, w1, gs, wb, offs, n1, n2, cand, cb, n3, n4):
    x_cand = unpack_weight(x_words, x_scales)[:, unstriped(cand)]
    xq = unpack_weight(x_words, x_scales)[:, unstriped(offs)]
    y = mxq(f64(w1), 0, "e4m3").T @ xq
    pa = y[:, unstriped(n1)]
    pb = y[:, unstriped(n2)]
    ra = np.maximum(pa, pb)
    ds = y.copy()
    ds[:, unstriped(n1)] = ra
    z = f64(gs) * ds
    a = 0.0625 * ((x_cand.T @ mxq(z, 0, "e4m3")))
    x_cb = unpack_weight(x_words, x_scales)[:, unstriped(cb)]
    b = x_cb.T @ mxq(f64(wb), 0, "e4m3")
    return (a + a[:, unstriped(n3)]) * (sigmoid(b + b[:, unstriped(n4)]))

@@ -1,0 +1,250 @@
+from contextlib import ExitStack
+
+import concourse.mybir as mybir
+from concourse.masks import make_identity
+
+F32 = mybir.dt.float32
+BF16 = mybir.dt.bfloat16
+I32 = mybir.dt.int32
+U32 = mybir.dt.uint32
+U16 = mybir.dt.uint16
+U8 = mybir.dt.uint8
+FP8X4 = mybir.dt.float8_e4m3fn_x4
+ALU = mybir.AluOpType
+ACT = mybir.ActivationFunctionType
+
+P = 128
+PACK = 4
+T = 2048
+S = 512
+W = 256
+TILES = 4
+FLOPS = 3 * 2 * 512 * 512 * 512
+
+
+def tile_picked_cdswtriebfill_none_p_kernel(
+    tc, x_words, x_scales, w1, gs, wb, offs, n1, n2, cand, cb, n3, n4, out
+):
+    nc = tc.nc
+    with ExitStack() as ctx:
+        lists = ctx.enter_context(tc.tile_pool(name="lists", bufs=1))
+        keep = ctx.enter_context(tc.tile_pool(name="keep", bufs=1))
+        psum = ctx.enter_context(tc.psum_pool(name="psum", bufs=2))
+
+        def load_list(name, src):
+            tile = lists.tile(list(src.shape), U16, name=name)
+            nc.sync.dma_start(tile[:], src)
+            return tile
+
+        def sb(name, shape, dtype, tag=None):
+            return keep.tile(shape, dtype, name=name, tag=tag or name, align_bytes=64)
+
+        xs = sb("xs", [P, T], U8)
+        nc.gpsimd.memset(xs[:].bitcast(I32), 0)
+        l_offs = load_list("l_offs", offs)
+        l_cand = load_list("l_cand", cand)
+        l_cb = load_list("l_cb", cb)
+        l_n1 = load_list("l_n1", n1)
+        l_n2 = load_list("l_n2", n2)
+        gain = sb("gain", [P, PACK], F32)
+        nc.sync.dma_start(gain[:], gs.rearrange("(p j) o -> p (j o)", j=PACK))
+        w1_rows = w1.rearrange("(p j) c -> p j c", j=PACK)
+        w1_raw = []
+        for h in range(2):
+            raw = sb(f"w1_raw{h}", [P, PACK, W], F32)
+            nc.sync.dma_start(raw[:], w1_rows[:, :, h * W : (h + 1) * W])
+            w1_raw.append(raw)
+        for q in range(4):
+            nc.sync.dma_start(xs[32 * q : 32 * q + 4, :].bitcast(I32), x_scales[0, 4 * q : 4 * q + 4, :].bitcast(I32))
+        xw = sb("xw", [P, T], I32)
+        nc.sync.dma_start(xw[:], x_words[0].rearrange("p c r -> p (c r)").bitcast(I32))
+        l_n4 = load_list("l_n4", n4)
+        l_n3 = load_list("l_n3", n3)
+        wb_raw = sb("wb_raw", [P, PACK, S], F32)
+        nc.sync.dma_start(wb_raw[:], wb.rearrange("(p j) c -> p j c", j=PACK))
+
+        ident = sb("ident", [P, P], F32)
+        make_identity(nc, ident[:])
+
+        def pick_scales(name, lst, tag=None):
+            picked = sb(name, [P, S], U8, tag)
+            nc.vector.tensor_copy(picked[:], xs[:].indirect(lst[:]))
+            return picked
+
+        def pick_words(name, lst, tag=None):
+            picked = sb(name, [P, S], U32, tag)
+            nc.vector.tensor_copy(picked[:], xw[:].bitcast(U32).indirect(lst[:]))
+            return picked
+
+        def mx(acc, lhs, lhs_s, rhs, rhs_s):
+            nc.tensor.matmul_mx(out=acc, lhsT=lhs.bitcast(FP8X4), lhsT_scale=lhs_s, rhs=rhs.bitcast(FP8X4),
+                                rhs_scale=rhs_s, start=True, stop=True)
+
+        def blk(i):
+            return slice(i * P, (i + 1) * P)
+
+        def half(h):
+            return slice(h * W, (h + 1) * W)
+
+        def half_list(lst, h):
+            return lst[:, h * (W // 16) : (h + 1) * (W // 16)]
+
+        sq = pick_scales("sq", l_offs)
+
+        w1_bf = sb("w1_bf", [P, S * PACK], BF16)
+        w1_view = w1_bf[:].rearrange("p (t m j) -> p m j t", t=TILES, j=PACK)
+        for h in range(2):
+            nc.scalar.copy(w1_view[:, h * 64 : (h + 1) * 64], w1_raw[h][:].rearrange("p j (m t) -> p m j t", t=TILES))
+        w1_q = [sb(f"w1_q{t}", [P, P], U32) for t in range(TILES)]
+        w1_s = [sb(f"w1_s{t}", [P, P], U8) for t in range(TILES)]
+        for t in range(TILES):
+            nc.vector.quantize_mx(out=w1_q[t][:].bitcast(FP8X4), scales=w1_s[t][:], in_=w1_bf[:, t * S : (t + 1) * S])
+
+        xq = pick_words("xq", l_offs)
+
+        ds = [sb(f"ds{t}", [P, S], F32) for t in range(TILES)]
+        pa = [sb(f"pa{t}", [P, W], F32) for t in range(TILES)]
+        pb = {}
+        ra = [sb(f"ra{t}", [P, W], F32) for t in range(TILES)]
+        z_pairs = sb("z_pairs", [P, 2, S, 2], BF16)
+
+        def y_product(t):
+            acc = psum.tile([P, S], F32, name="ya")
+            mx(acc[:], w1_q[t][:], w1_s[t][:], xq[:], sq[:])
+            nc.scalar.copy(ds[t][:], acc[:])
+
+        def y_fetch(t, tag=None):
+            pb[t] = sb(f"pb{t}", [P, W], F32, tag)
+            nc.scalar.activation(pa[t][:], ds[t][:].indirect(l_n1[:]), ACT.Copy)
+            nc.vector.tensor_copy(pb[t][:], ds[t][:].indirect(l_n2[:]))
+            nc.vector.tensor_tensor(ra[t][:], pa[t][:], pb[t][:], ALU.max)
+
+        def y_put(t):
+            nc.scalar.activation(ds[t][:].indirect(l_n1[:]), ra[t][:], ACT.Copy)
+
+        def z_round(t):
+            nc.vector.tensor_scalar(z_pairs[:, t // 2, :, t % 2], ds[t][:], gain[:, t : t + 1], None, ALU.mult)
+
+        b_sb = {}
+        gb = {}
+        th = [sb(f"th{i}", [P, S], F32) for i in range(TILES)]
+        wb_q = sb("wb_q", [P, S], U32)
+        wb_s = sb("wb_s", [P, S], U8)
+
+        def b_product(i, on_scalar, tag=None):
+            b_sb[i] = sb(f"b_sb{i}", [P, S], F32, tag)
+            acc = psum.tile([P, S], F32, name="bacc")
+            mx(acc[:], xb[:, blk(i)], sbb[:, blk(i)], wb_q[:], wb_s[:])
+            if on_scalar:
+                nc.scalar.copy(b_sb[i][:], acc[:])
+            else:
+                nc.vector.tensor_copy(b_sb[i][:], acc[:])
+
+        def b_fetch(i, on_scalar, tag=None):
+            gb[i] = sb(f"gb{i}", [P, S], F32, tag)
+            for h in range(2):
+                window = b_sb[i][:].indirect(half_list(l_n4, h))
+                if on_scalar:
+                    nc.scalar.activation(gb[i][:, half(h)], window, ACT.Copy)
+                else:
+                    nc.vector.tensor_copy(gb[i][:, half(h)], window)
+
+        def b_gate(i):
+            sum_t = psum.tile([P, S], F32, name="sum_t")
+            for j in range(TILES):
+                nc.tensor.matmul(sum_t[:, blk(j)], b_sb[i][:, blk(j)], ident[:], is_transpose=True, start=True, stop=False)
+                nc.tensor.matmul(sum_t[:, blk(j)], gb[i][:, blk(j)], ident[:], is_transpose=True, start=False, stop=True)
+            nc.scalar.activation(th[i][:], sum_t[:], ACT.Tanh, scale=0.5)
+
+        xc = pick_words("xc", l_cand)
+        y_product(0)
+        y_product(1)
+        sc = pick_scales("sc", l_cand, "w1_q0")
+        y_fetch(0)
+        y_fetch(1)
+        xb = pick_words("xb", l_cb, "pa0")
+        y_product(2)
+        y_put(0)
+        sbb = pick_scales("sbb", l_cb, "pb0")
+        wb_bf = sb("wb_bf", [P, S * PACK], BF16, "pa1")
+        nc.vector.tensor_copy(
+            wb_bf[:].rearrange("p (c i j) -> p c j i", i=4, j=PACK),
+            wb_raw[:].rearrange("p j (c i) -> p c j i", i=4),
+        )
+        y_fetch(2, "wb_raw")
+        y_product(3)
+        y_put(1)
+        nc.vector.quantize_mx(out=wb_q[:].bitcast(FP8X4), scales=wb_s[:], in_=wb_bf[:])
+        z_round(0)
+        y_fetch(3, "pa1")
+        y_put(2)
+        z_round(1)
+        y_put(3)
+        b_product(0, False)
+        z_round(2)
+        b_product(1, False)
+        z_round(3)
+        b_fetch(0, True)
+        b_fetch(1, True)
+
+        z_bf = sb("z_bf", [P, S * PACK], BF16)
+        z_q = sb("z_q", [P, S], U32)
+        z_s = sb("z_s", [P, S], U8)
+        z_words = z_bf[:].bitcast(I32).rearrange("p (c u) -> p c u", u=2)
+        pair_words = z_pairs[:].rearrange("p u c e -> p (u c e)").bitcast(I32).rearrange("p (u c) -> p c u", u=2)
+        for h in range(2):
+            nc.vector.tensor_copy(z_words[:, half(h)], pair_words[:, half(h)])
+        for h in range(2):
+            nc.vector.quantize_mx(out=z_q[:, half(h)].bitcast(FP8X4), scales=z_s[:, half(h)],
+                                  in_=z_bf[:, h * W * PACK : (h + 1) * W * PACK])
+
+        b_product(2, False, "z_pairs")
+        b_product(3, False, "z_bf")
+
+        a_sb = [sb(f"a_sb{i}", [P, S], F32) for i in range(TILES)]
+        ga = [sb(f"ga{i}", [P, S], F32) for i in range(TILES)]
+        asum = [sb(f"asum{i}", [P, S], F32) for i in range(TILES)]
+        res = [sb(f"res{i}", [P, S], F32) for i in range(TILES)]
+
+        def a_product(i, on_scalar):
+            acc = psum.tile([P, S], F32, name="ya")
+            for h in range(2):
+                mx(acc[:, half(h)], xc[:, blk(i)], sc[:, blk(i)], z_q[:, half(h)], z_s[:, half(h)])
+            if on_scalar:
+                nc.scalar.activation(a_sb[i][:], acc[:], ACT.Copy, scale=0.03125)
+            else:
+                nc.vector.tensor_scalar(a_sb[i][:], acc[:], 0.03125, None, ALU.mult)
+
+        def a_fetch(i):
+            for h in range(2):
+                nc.scalar.activation(ga[i][:, half(h)], a_sb[i][:].indirect(half_list(l_n3, h)), ACT.Copy)
+
+        def finish(i, pieces):
+            back = psum.tile([P, S], F32, name="back")
+            for j in range(TILES):
+                nc.tensor.transpose(back[:, blk(j)], th[i][:, blk(j)], ident[:])
+            for cols in pieces:
+                nc.vector.tensor_tensor(asum[i][:, cols], a_sb[i][:, cols], ga[i][:, cols], ALU.add)
+            for cols in pieces:
+                nc.vector.scalar_tensor_tensor(res[i][:, cols], back[:, cols], 1.0, asum[i][:, cols], ALU.add, ALU.mult)
+                nc.sync.dma_start(out[blk(i), cols], res[i][:, cols])
+
+        whole = [slice(0, S)]
+        a_product(0, True)
+        a_product(1, False)
+        a_fetch(0)
+        b_gate(0)
+        b_fetch(2, False)
+        a_product(2, False)
+        a_fetch(1)
+        b_gate(1)
+        finish(0, whole)
+        b_fetch(3, False)
+        a_product(3, False)
+        a_fetch(2)
+        b_gate(2)
+        finish(1, whole)
+        b_gate(3)
+        a_fetch(3)
+        finish(2, whole)
+        finish(3, [half(0), half(1)])

@@ -29,7 +29,7 @@ def tile_picked_cdswtriebfill_none_p_kernel(
     with ExitStack() as ctx:
         lists = ctx.enter_context(tc.tile_pool(name="lists", bufs=1))
         keep = ctx.enter_context(tc.tile_pool(name="keep", bufs=1))
-        psum = ctx.enter_context(tc.psum_pool(name="psum", bufs=2))
+        psum = ctx.enter_context(tc.psum_pool(name="psum", bufs=1))
 
         def load_list(name, src):
             tile = lists.tile(list(src.shape), U16, name=name)
@@ -44,24 +44,20 @@ def tile_picked_cdswtriebfill_none_p_kernel(
         l_offs = load_list("l_offs", offs)
         l_cand = load_list("l_cand", cand)
         l_cb = load_list("l_cb", cb)
+        for q in range(4):
+            nc.sync.dma_start(xs[32 * q : 32 * q + 4, :].bitcast(I32), x_scales[0, 4 * q : 4 * q + 4, :].bitcast(I32))
+        w1_raw = sb("w1_raw", [P, PACK, S], F32)
+        nc.sync.dma_start(w1_raw[:], w1.rearrange("(p j) c -> p j c", j=PACK))
+        xw = sb("xw", [P, T], I32)
+        nc.sync.dma_start(xw[:], x_words[0].rearrange("p c r -> p (c r)").bitcast(I32))
         l_n1 = load_list("l_n1", n1)
+        wb_raw = sb("wb_raw", [P, PACK, S], F32)
+        nc.sync.dma_start(wb_raw[:], wb.rearrange("(p j) c -> p j c", j=PACK))
         l_n2 = load_list("l_n2", n2)
         gain = sb("gain", [P, PACK], F32)
         nc.sync.dma_start(gain[:], gs.rearrange("(p j) o -> p (j o)", j=PACK))
-        w1_rows = w1.rearrange("(p j) c -> p j c", j=PACK)
-        w1_raw = []
-        for h in range(2):
-            raw = sb(f"w1_raw{h}", [P, PACK, W], F32)
-            nc.sync.dma_start(raw[:], w1_rows[:, :, h * W : (h + 1) * W])
-            w1_raw.append(raw)
-        for q in range(4):
-            nc.sync.dma_start(xs[32 * q : 32 * q + 4, :].bitcast(I32), x_scales[0, 4 * q : 4 * q + 4, :].bitcast(I32))
-        xw = sb("xw", [P, T], I32)
-        nc.sync.dma_start(xw[:], x_words[0].rearrange("p c r -> p (c r)").bitcast(I32))
         l_n4 = load_list("l_n4", n4)
         l_n3 = load_list("l_n3", n3)
-        wb_raw = sb("wb_raw", [P, PACK, S], F32)
-        nc.sync.dma_start(wb_raw[:], wb.rearrange("(p j) c -> p j c", j=PACK))
 
         ident = sb("ident", [P, P], F32)
         make_identity(nc, ident[:])
@@ -80,6 +76,9 @@ def tile_picked_cdswtriebfill_none_p_kernel(
             nc.tensor.matmul_mx(out=acc, lhsT=lhs.bitcast(FP8X4), lhsT_scale=lhs_s, rhs=rhs.bitcast(FP8X4),
                                 rhs_scale=rhs_s, start=True, stop=True)
 
+        def bank(name, b):
+            return psum.tile([P, S], F32, name=name, tag=f"bank{b}")
+
         def blk(i):
             return slice(i * P, (i + 1) * P)
 
@@ -90,17 +89,25 @@ def tile_picked_cdswtriebfill_none_p_kernel(
             return lst[:, h * (W // 16) : (h + 1) * (W // 16)]
 
         sq = pick_scales("sq", l_offs)
+        sc = pick_scales("sc", l_cand)
+        sbb = pick_scales("sbb", l_cb)
 
-        w1_bf = sb("w1_bf", [P, S * PACK], BF16)
-        w1_view = w1_bf[:].rearrange("p (t m j) -> p m j t", t=TILES, j=PACK)
+        w1_cols = w1_raw[:].rearrange("p j (m t) -> p m j t", t=TILES)
+        w1_bf = [sb(f"w1_bf{h}", [P, 2, P * PACK], BF16) for h in range(2)]
         for h in range(2):
-            nc.scalar.copy(w1_view[:, h * 64 : (h + 1) * 64], w1_raw[h][:].rearrange("p j (m t) -> p m j t", t=TILES))
-        w1_q = [sb(f"w1_q{t}", [P, P], U32) for t in range(TILES)]
-        w1_s = [sb(f"w1_s{t}", [P, P], U8) for t in range(TILES)]
-        for t in range(TILES):
-            nc.vector.quantize_mx(out=w1_q[t][:].bitcast(FP8X4), scales=w1_s[t][:], in_=w1_bf[:, t * S : (t + 1) * S])
+            nc.scalar.copy(w1_bf[h][:].rearrange("p t (m j) -> p m j t", j=PACK), w1_cols[:, :, :, 2 * h : 2 * h + 2])
+        w1_q, w1_s = {}, {}
 
-        xq = pick_words("xq", l_offs)
+        def w1_quantise(t, tag=None):
+            w1_q[t] = sb(f"w1_q{t}", [P, P], U32, tag)
+            w1_s[t] = sb(f"w1_s{t}", [P, P], U8)
+            nc.vector.quantize_mx(out=w1_q[t][:].bitcast(FP8X4), scales=w1_s[t][:], in_=w1_bf[t // 2][:, t % 2, :])
+
+        w1_quantise(0)
+        w1_quantise(1)
+        xq = sb("xq", [P, S], U32, "w1_bf0")
+        for h in range(2):
+            nc.vector.tensor_copy(xq[:, half(h)], xw[:].bitcast(U32).indirect(half_list(l_offs, h)))
 
         ds = [sb(f"ds{t}", [P, S], F32) for t in range(TILES)]
         pa = [sb(f"pa{t}", [P, W], F32) for t in range(TILES)]
@@ -108,14 +115,21 @@ def tile_picked_cdswtriebfill_none_p_kernel(
         ra = [sb(f"ra{t}", [P, W], F32) for t in range(TILES)]
         z_pairs = sb("z_pairs", [P, 2, S, 2], BF16)
 
+        y_acc = {}
+
         def y_product(t):
-            acc = psum.tile([P, S], F32, name="ya")
-            mx(acc[:], w1_q[t][:], w1_s[t][:], xq[:], sq[:])
-            nc.scalar.copy(ds[t][:], acc[:])
+            y_acc[t] = bank(f"y_acc{t}", t)
+            for cols in ([half(0), half(1)] if t == 0 else [slice(0, S)]):
+                mx(y_acc[t][:, cols], w1_q[t][:], w1_s[t][:], xq[:, cols], sq[:, cols])
+
+        def y_copy(t):
+            nc.scalar.copy(ds[t][:], y_acc[t][:])
+
+        def y_first(t):
+            nc.scalar.activation(pa[t][:], ds[t][:].indirect(l_n1[:]), ACT.Copy)
 
         def y_fetch(t, tag=None):
             pb[t] = sb(f"pb{t}", [P, W], F32, tag)
-            nc.scalar.activation(pa[t][:], ds[t][:].indirect(l_n1[:]), ACT.Copy)
             nc.vector.tensor_copy(pb[t][:], ds[t][:].indirect(l_n2[:]))
             nc.vector.tensor_tensor(ra[t][:], pa[t][:], pb[t][:], ALU.max)
 
@@ -123,7 +137,8 @@ def tile_picked_cdswtriebfill_none_p_kernel(
             nc.scalar.activation(ds[t][:].indirect(l_n1[:]), ra[t][:], ACT.Copy)
 
         def z_round(t):
-            nc.vector.tensor_scalar(z_pairs[:, t // 2, :, t % 2], ds[t][:], gain[:, t : t + 1], None, ALU.mult)
+            for cols in ([half(0), half(1)] if t == TILES - 1 else [slice(0, S)]):
+                nc.vector.tensor_scalar(z_pairs[:, t // 2, cols, t % 2], ds[t][:, cols], gain[:, t : t + 1], None, ALU.mult)
 
         b_sb = {}
         gb = {}
@@ -133,59 +148,65 @@ def tile_picked_cdswtriebfill_none_p_kernel(
 
         def b_product(i, on_scalar, tag=None):
             b_sb[i] = sb(f"b_sb{i}", [P, S], F32, tag)
-            acc = psum.tile([P, S], F32, name="bacc")
+            acc = bank(f"b_acc{i}", i)
             mx(acc[:], xb[:, blk(i)], sbb[:, blk(i)], wb_q[:], wb_s[:])
             if on_scalar:
                 nc.scalar.copy(b_sb[i][:], acc[:])
             else:
                 nc.vector.tensor_copy(b_sb[i][:], acc[:])
 
-        def b_fetch(i, on_scalar, tag=None):
+        def b_fetch(i, halves_on_scalar, tag=None):
             gb[i] = sb(f"gb{i}", [P, S], F32, tag)
             for h in range(2):
                 window = b_sb[i][:].indirect(half_list(l_n4, h))
-                if on_scalar:
+                if h in halves_on_scalar:
                     nc.scalar.activation(gb[i][:, half(h)], window, ACT.Copy)
                 else:
                     nc.vector.tensor_copy(gb[i][:, half(h)], window)
 
         def b_gate(i):
-            sum_t = psum.tile([P, S], F32, name="sum_t")
+            sum_t = bank(f"sum_t{i}", 4 + i)
             for j in range(TILES):
                 nc.tensor.matmul(sum_t[:, blk(j)], b_sb[i][:, blk(j)], ident[:], is_transpose=True, start=True, stop=False)
                 nc.tensor.matmul(sum_t[:, blk(j)], gb[i][:, blk(j)], ident[:], is_transpose=True, start=False, stop=True)
             nc.scalar.activation(th[i][:], sum_t[:], ACT.Tanh, scale=0.5)
 
-        xc = pick_words("xc", l_cand)
+        xc = pick_words("xc", l_cand, "w1_raw")
         y_product(0)
         y_product(1)
-        sc = pick_scales("sc", l_cand, "w1_q0")
-        y_fetch(0)
-        y_fetch(1)
-        xb = pick_words("xb", l_cb, "pa0")
+        w1_quantise(2, "w1_q0")
+        w1_quantise(3, "w1_q1")
         y_product(2)
-        y_put(0)
-        sbb = pick_scales("sbb", l_cb, "pb0")
-        wb_bf = sb("wb_bf", [P, S * PACK], BF16, "pa1")
+        y_product(3)
+        for t in (0, 2):
+            y_copy(t)
+            y_copy(t + 1)
+            y_first(t)
+            y_first(t + 1)
+        wb_bf = sb("wb_bf", [P, S * PACK], BF16)
         nc.vector.tensor_copy(
             wb_bf[:].rearrange("p (c i j) -> p c j i", i=4, j=PACK),
             wb_raw[:].rearrange("p j (c i) -> p c j i", i=4),
         )
-        y_fetch(2, "wb_raw")
-        y_product(3)
-        y_put(1)
+        y_fetch(0)
         nc.vector.quantize_mx(out=wb_q[:].bitcast(FP8X4), scales=wb_s[:], in_=wb_bf[:])
-        z_round(0)
-        y_fetch(3, "pa1")
-        y_put(2)
-        z_round(1)
-        y_put(3)
+        xb = pick_words("xb", l_cb, "pa0")
+        y_fetch(1)
+        y_fetch(2)
         b_product(0, False)
-        z_round(2)
+        y_fetch(3)
+        for t in range(TILES):
+            y_put(t)
         b_product(1, False)
+        b_fetch(0, ())
+        z_round(0)
+        z_round(1)
+        z_round(2)
+        b_fetch(1, (1,))
         z_round(3)
-        b_fetch(0, True)
-        b_fetch(1, True)
+        b_gate(0)
+        b_product(2, True, "ra3")
+        b_product(3, True, "ds3")
 
         z_bf = sb("z_bf", [P, S * PACK], BF16)
         z_q = sb("z_q", [P, S], U32)
@@ -198,29 +219,31 @@ def tile_picked_cdswtriebfill_none_p_kernel(
             nc.vector.quantize_mx(out=z_q[:, half(h)].bitcast(FP8X4), scales=z_s[:, half(h)],
                                   in_=z_bf[:, h * W * PACK : (h + 1) * W * PACK])
 
-        b_product(2, False, "z_pairs")
-        b_product(3, False, "z_bf")
 
         a_sb = [sb(f"a_sb{i}", [P, S], F32) for i in range(TILES)]
         ga = [sb(f"ga{i}", [P, S], F32) for i in range(TILES)]
         asum = [sb(f"asum{i}", [P, S], F32) for i in range(TILES)]
         res = [sb(f"res{i}", [P, S], F32) for i in range(TILES)]
 
-        def a_product(i, on_scalar):
-            acc = psum.tile([P, S], F32, name="ya")
-            for h in range(2):
-                mx(acc[:, half(h)], xc[:, blk(i)], sc[:, blk(i)], z_q[:, half(h)], z_s[:, half(h)])
+        a_acc = {}
+
+        def a_product(i):
+            a_acc[i] = bank(f"a_acc{i}", (6 + i) % 8)
+            for cols in ([half(0), half(1)] if i == 0 else [slice(0, S)]):
+                mx(a_acc[i][:, cols], xc[:, blk(i)], sc[:, blk(i)], z_q[:, cols], z_s[:, cols])
+
+        def a_copy(i, on_scalar):
             if on_scalar:
-                nc.scalar.activation(a_sb[i][:], acc[:], ACT.Copy, scale=0.03125)
+                nc.scalar.activation(a_sb[i][:], a_acc[i][:], ACT.Copy, scale=0.03125)
             else:
-                nc.vector.tensor_scalar(a_sb[i][:], acc[:], 0.03125, None, ALU.mult)
+                nc.vector.tensor_scalar(a_sb[i][:], a_acc[i][:], 0.03125, None, ALU.mult)
 
         def a_fetch(i):
             for h in range(2):
                 nc.scalar.activation(ga[i][:, half(h)], a_sb[i][:].indirect(half_list(l_n3, h)), ACT.Copy)
 
         def finish(i, pieces):
-            back = psum.tile([P, S], F32, name="back")
+            back = bank(f"back{i}", i)
             for j in range(TILES):
                 nc.tensor.transpose(back[:, blk(j)], th[i][:, blk(j)], ident[:])
             for cols in pieces:
@@ -230,21 +253,22 @@ def tile_picked_cdswtriebfill_none_p_kernel(
                 nc.sync.dma_start(out[blk(i), cols], res[i][:, cols])
 
         whole = [slice(0, S)]
-        a_product(0, True)
-        a_product(1, False)
+        for i in range(TILES):
+            a_product(i)
+        b_fetch(2, (), "z_pairs")
+        a_copy(0, True)
+        a_copy(1, False)
+        b_fetch(3, (), "z_bf")
         a_fetch(0)
-        b_gate(0)
-        b_fetch(2, False)
-        a_product(2, False)
-        a_fetch(1)
         b_gate(1)
-        finish(0, whole)
-        b_fetch(3, False)
-        a_product(3, False)
-        a_fetch(2)
+        a_copy(2, False)
+        a_fetch(1)
         b_gate(2)
-        finish(1, whole)
+        finish(0, whole)
+        a_copy(3, False)
+        a_fetch(2)
         b_gate(3)
+        finish(1, whole)
         a_fetch(3)
         finish(2, whole)
         finish(3, [half(0), half(1)])

@@ -112,8 +112,7 @@ def tile_picked_cdswtriebfill_none_p_kernel(
         ds = [sb(f"ds{t}", [P, S], F32) for t in range(TILES)]
         pa = [sb(f"pa{t}", [P, W], F32) for t in range(TILES)]
         pb = {}
-        ra = [sb(f"ra{t}", [P, W], F32) for t in range(TILES)]
-        z_pairs = sb("z_pairs", [P, 2, S, 2], BF16)
+        ra = {}
 
         y_acc = {}
 
@@ -128,9 +127,12 @@ def tile_picked_cdswtriebfill_none_p_kernel(
         def y_first(t):
             nc.scalar.activation(pa[t][:], ds[t][:].indirect(l_n1[:]), ACT.Copy)
 
-        def y_fetch(t, tag=None):
-            pb[t] = sb(f"pb{t}", [P, W], F32, tag)
+        def y_second(t):
+            pb[t] = sb(f"pb{t}", [P, W], F32)
             nc.vector.tensor_copy(pb[t][:], ds[t][:].indirect(l_n2[:]))
+
+        def y_larger(t, tag=None):
+            ra[t] = sb(f"ra{t}", [P, W], F32, tag)
             nc.vector.tensor_tensor(ra[t][:], pa[t][:], pb[t][:], ALU.max)
 
         def y_put(t):
@@ -143,39 +145,43 @@ def tile_picked_cdswtriebfill_none_p_kernel(
         b_sb = {}
         gb = {}
         th = [sb(f"th{i}", [P, S], F32) for i in range(TILES)]
-        wb_q = sb("wb_q", [P, S], U32)
         wb_s = sb("wb_s", [P, S], U8)
 
         def b_product(i, on_scalar, tag=None):
             b_sb[i] = sb(f"b_sb{i}", [P, S], F32, tag)
             acc = bank(f"b_acc{i}", i)
-            mx(acc[:], xb[:, blk(i)], sbb[:, blk(i)], wb_q[:], wb_s[:])
+            for cols in ([half(0), half(1)] if i == 0 else [slice(0, S)]):
+                mx(acc[:, cols], xb[:, blk(i)], sbb[:, blk(i)], wb_q[:, cols], wb_s[:, cols])
             if on_scalar:
                 nc.scalar.copy(b_sb[i][:], acc[:])
             else:
                 nc.vector.tensor_copy(b_sb[i][:], acc[:])
 
-        def b_fetch(i, halves_on_scalar, tag=None):
-            gb[i] = sb(f"gb{i}", [P, S], F32, tag)
+        def b_fetch_half(i, h, on_scalar, dst):
+            gb[i, h] = dst
+            window = b_sb[i][:].indirect(half_list(l_n4, h))
+            if on_scalar:
+                nc.scalar.activation(dst, window, ACT.Copy)
+            else:
+                nc.vector.tensor_copy(dst, window)
+
+        def b_fetch(i, on_scalar, tag=None):
+            fetched = sb(f"gb{i}", [P, S], F32, tag)
             for h in range(2):
-                window = b_sb[i][:].indirect(half_list(l_n4, h))
-                if h in halves_on_scalar:
-                    nc.scalar.activation(gb[i][:, half(h)], window, ACT.Copy)
-                else:
-                    nc.vector.tensor_copy(gb[i][:, half(h)], window)
+                b_fetch_half(i, h, on_scalar, fetched[:, half(h)])
 
         def b_gate(i):
             sum_t = bank(f"sum_t{i}", 4 + i)
             for j in range(TILES):
                 nc.tensor.matmul(sum_t[:, blk(j)], b_sb[i][:, blk(j)], ident[:], is_transpose=True, start=True, stop=False)
-                nc.tensor.matmul(sum_t[:, blk(j)], gb[i][:, blk(j)], ident[:], is_transpose=True, start=False, stop=True)
+                nc.tensor.matmul(sum_t[:, blk(j)], gb[i, j // 2][:, blk(j % 2)], ident[:], is_transpose=True, start=False, stop=True)
             nc.scalar.activation(th[i][:], sum_t[:], ACT.Tanh, scale=0.5)
 
         xc = pick_words("xc", l_cand, "w1_raw")
         y_product(0)
         y_product(1)
         w1_quantise(2, "w1_q0")
-        w1_quantise(3, "w1_q1")
+        w1_quantise(3, "w1_s0")
         y_product(2)
         y_product(3)
         for t in (0, 2):
@@ -183,30 +189,37 @@ def tile_picked_cdswtriebfill_none_p_kernel(
             y_copy(t + 1)
             y_first(t)
             y_first(t + 1)
-        wb_bf = sb("wb_bf", [P, S * PACK], BF16)
-        nc.vector.tensor_copy(
-            wb_bf[:].rearrange("p (c i j) -> p c j i", i=4, j=PACK),
-            wb_raw[:].rearrange("p j (c i) -> p c j i", i=4),
-        )
-        y_fetch(0)
-        nc.vector.quantize_mx(out=wb_q[:].bitcast(FP8X4), scales=wb_s[:], in_=wb_bf[:])
-        xb = pick_words("xb", l_cb, "pa0")
-        y_fetch(1)
-        y_fetch(2)
-        b_product(0, False)
-        y_fetch(3)
+        wb_cols = wb_raw[:].rearrange("p j c -> p c j")
+        wb_bf = [sb(f"wb_bf{h}", [P, W, PACK], BF16, tag) for h, tag in enumerate(("w1_bf1", "w1_q0"))]
+        for h in range(2):
+            nc.gpsimd.tensor_scalar(wb_bf[h][:], wb_cols[:, half(h)], 1.0, 0.0, ALU.mult, ALU.add)
+        xb = pick_words("xb", l_cb, "w1_q1")
+        for t in range(TILES):
+            y_second(t)
+        y_larger(0)
+        y_larger(1)
+        wb_q = sb("wb_q", [P, S], U32, "wb_raw")
+        for h in range(2):
+            nc.vector.quantize_mx(out=wb_q[:, half(h)].bitcast(FP8X4), scales=wb_s[:, half(h)],
+                                  in_=wb_bf[h][:].rearrange("p c j -> p (c j)"))
+        y_larger(2, "w1_bf1")
+        y_larger(3, "w1_q0")
+        z_pairs = sb("z_pairs", [P, 2, S, 2], BF16, "pa3")
         for t in range(TILES):
             y_put(t)
+        b_product(0, False)
         b_product(1, False)
-        b_fetch(0, ())
+        b_fetch(0, False)
         z_round(0)
         z_round(1)
+        b_fetch(1, False)
         z_round(2)
-        b_fetch(1, (1,))
+        b_product(2, False)
         z_round(3)
+        b_product(3, True, "pb2")
+        b_fetch_half(2, 0, True, sb("gb2a", [P, W], F32, "w1_q0")[:])
         b_gate(0)
-        b_product(2, True, "ra3")
-        b_product(3, True, "ds3")
+        b_gate(1)
 
         z_bf = sb("z_bf", [P, S * PACK], BF16)
         z_q = sb("z_q", [P, S], U32)
@@ -222,27 +235,33 @@ def tile_picked_cdswtriebfill_none_p_kernel(
 
         a_sb = [sb(f"a_sb{i}", [P, S], F32) for i in range(TILES)]
         ga = [sb(f"ga{i}", [P, S], F32) for i in range(TILES)]
-        asum = [sb(f"asum{i}", [P, S], F32) for i in range(TILES)]
+        asum = {}
         res = [sb(f"res{i}", [P, S], F32) for i in range(TILES)]
 
         a_acc = {}
 
         def a_product(i):
-            a_acc[i] = bank(f"a_acc{i}", (6 + i) % 8)
-            for cols in ([half(0), half(1)] if i == 0 else [slice(0, S)]):
-                mx(a_acc[i][:, cols], xc[:, blk(i)], sc[:, blk(i)], z_q[:, cols], z_s[:, cols])
+            pieces = [(half(0), 2), (half(1), 6)] if i == 0 else [(slice(0, S), (6 + i) % 8)]
+            a_acc[i] = []
+            for cols, b in pieces:
+                acc = bank(f"a_acc{i}_{b}", b)
+                mx(acc[:, cols], xc[:, blk(i)], sc[:, blk(i)], z_q[:, cols], z_s[:, cols])
+                a_acc[i].append((cols, acc))
 
         def a_copy(i, on_scalar):
-            if on_scalar:
-                nc.scalar.activation(a_sb[i][:], a_acc[i][:], ACT.Copy, scale=0.03125)
-            else:
-                nc.vector.tensor_scalar(a_sb[i][:], a_acc[i][:], 0.03125, None, ALU.mult)
+            for cols, acc in a_acc[i]:
+                if on_scalar:
+                    nc.scalar.activation(a_sb[i][:, cols], acc[:, cols], ACT.Copy, scale=0.03125)
+                else:
+                    nc.vector.tensor_scalar(a_sb[i][:, cols], acc[:, cols], 0.03125, None, ALU.mult)
 
-        def a_fetch(i):
-            for h in range(2):
-                nc.scalar.activation(ga[i][:, half(h)], a_sb[i][:].indirect(half_list(l_n3, h)), ACT.Copy)
+        def a_fetch(i, pieces):
+            for cols in pieces:
+                offsets = l_n3[:, cols.start // 16 : cols.stop // 16]
+                nc.scalar.activation(ga[i][:, cols], a_sb[i][:].indirect(offsets), ACT.Copy)
 
-        def finish(i, pieces):
+        def finish(i, pieces, tag=None):
+            asum[i] = sb(f"asum{i}", [P, S], F32, tag)
             back = bank(f"back{i}", i)
             for j in range(TILES):
                 nc.tensor.transpose(back[:, blk(j)], th[i][:, blk(j)], ident[:])
@@ -253,22 +272,23 @@ def tile_picked_cdswtriebfill_none_p_kernel(
                 nc.sync.dma_start(out[blk(i), cols], res[i][:, cols])
 
         whole = [slice(0, S)]
+        halves = [half(0), half(1)]
+        last = [half(0), blk(2), blk(3)]
         for i in range(TILES):
             a_product(i)
-        b_fetch(2, (), "z_pairs")
+        b_fetch_half(2, 1, False, sb("gb2b", [P, W], F32, "pa3")[:])
+        b_fetch(3, False, "z_bf")
         a_copy(0, True)
         a_copy(1, False)
-        b_fetch(3, (), "z_bf")
-        a_fetch(0)
-        b_gate(1)
+        a_fetch(0, halves)
         a_copy(2, False)
-        a_fetch(1)
+        a_fetch(1, halves)
         b_gate(2)
-        finish(0, whole)
         a_copy(3, False)
-        a_fetch(2)
+        finish(0, whole)
+        a_fetch(2, halves)
         b_gate(3)
         finish(1, whole)
-        a_fetch(3)
+        a_fetch(3, last)
         finish(2, whole)
-        finish(3, [half(0), half(1)])
+        finish(3, last, "asum2")

@@ -144,14 +144,13 @@ def tile_picked_cdswtriebfill_none_p_kernel(
 
         b_sb = {}
         gb = {}
-        th = [sb(f"th{i}", [P, S], F32) for i in range(TILES)]
+        th = {}
         wb_s = sb("wb_s", [P, S], U8)
 
         def b_product(i, on_scalar, tag=None):
             b_sb[i] = sb(f"b_sb{i}", [P, S], F32, tag)
             acc = bank(f"b_acc{i}", i)
-            for cols in ([half(0), half(1)] if i == 0 else [slice(0, S)]):
-                mx(acc[:, cols], xb[:, blk(i)], sbb[:, blk(i)], wb_q[:, cols], wb_s[:, cols])
+            mx(acc[:], xb[:, blk(i)], sbb[:, blk(i)], wb_q[:], wb_s[:])
             if on_scalar:
                 nc.scalar.copy(b_sb[i][:], acc[:])
             else:
@@ -170,7 +169,8 @@ def tile_picked_cdswtriebfill_none_p_kernel(
             for h in range(2):
                 b_fetch_half(i, h, on_scalar, fetched[:, half(h)])
 
-        def b_gate(i):
+        def b_gate(i, tag=None):
+            th[i] = sb(f"th{i}", [P, S], F32, tag)
             sum_t = bank(f"sum_t{i}", 4 + i)
             for j in range(TILES):
                 nc.tensor.matmul(sum_t[:, blk(j)], b_sb[i][:, blk(j)], ident[:], is_transpose=True, start=True, stop=False)
@@ -189,21 +189,22 @@ def tile_picked_cdswtriebfill_none_p_kernel(
             y_copy(t + 1)
             y_first(t)
             y_first(t + 1)
-        wb_cols = wb_raw[:].rearrange("p j c -> p c j")
-        wb_bf = [sb(f"wb_bf{h}", [P, W, PACK], BF16, tag) for h, tag in enumerate(("w1_bf1", "w1_q0"))]
-        for h in range(2):
-            nc.gpsimd.tensor_scalar(wb_bf[h][:], wb_cols[:, half(h)], 1.0, 0.0, ALU.mult, ALU.add)
-        xb = pick_words("xb", l_cb, "w1_q1")
-        for t in range(TILES):
-            y_second(t)
+        wb_bf = sb("wb_bf", [P, S * PACK], BF16)
+        wb_q = sb("wb_q", [P, S], U32)
+        nc.vector.tensor_copy(
+            wb_bf[:].rearrange("p (c i j) -> p c j i", i=4, j=PACK),
+            wb_raw[:].rearrange("p j (c i) -> p c j i", i=4),
+        )
+        y_second(0)
+        y_second(1)
+        nc.vector.quantize_mx(out=wb_q[:].bitcast(FP8X4), scales=wb_s[:], in_=wb_bf[:])
         y_larger(0)
         y_larger(1)
-        wb_q = sb("wb_q", [P, S], U32, "wb_raw")
-        for h in range(2):
-            nc.vector.quantize_mx(out=wb_q[:, half(h)].bitcast(FP8X4), scales=wb_s[:, half(h)],
-                                  in_=wb_bf[h][:].rearrange("p c j -> p (c j)"))
-        y_larger(2, "w1_bf1")
-        y_larger(3, "w1_q0")
+        xb = pick_words("xb", l_cb, "pa0")
+        y_second(2)
+        y_second(3)
+        y_larger(2)
+        y_larger(3)
         z_pairs = sb("z_pairs", [P, 2, S, 2], BF16, "pa3")
         for t in range(TILES):
             y_put(t)
@@ -212,14 +213,13 @@ def tile_picked_cdswtriebfill_none_p_kernel(
         b_fetch(0, False)
         z_round(0)
         z_round(1)
-        b_fetch(1, False)
         z_round(2)
-        b_product(2, False)
+        b_fetch_half(1, 0, False, sb("gb1a", [P, W], F32)[:])
         z_round(3)
-        b_product(3, True, "pb2")
-        b_fetch_half(2, 0, True, sb("gb2a", [P, W], F32, "w1_q0")[:])
+        b_fetch_half(1, 1, True, sb("gb1b", [P, W], F32)[:])
+        b_product(2, True, "ds2")
+        b_product(3, True, "ds3")
         b_gate(0)
-        b_gate(1)
 
         z_bf = sb("z_bf", [P, S * PACK], BF16)
         z_q = sb("z_q", [P, S], U32)
@@ -260,13 +260,15 @@ def tile_picked_cdswtriebfill_none_p_kernel(
                 offsets = l_n3[:, cols.start // 16 : cols.stop // 16]
                 nc.scalar.activation(ga[i][:, cols], a_sb[i][:].indirect(offsets), ACT.Copy)
 
-        def finish(i, pieces, tag=None):
-            asum[i] = sb(f"asum{i}", [P, S], F32, tag)
+        def a_sum(i, pieces):
+            asum[i] = sb(f"asum{i}", [P, S], F32)
+            for cols in pieces:
+                nc.vector.tensor_tensor(asum[i][:, cols], a_sb[i][:, cols], ga[i][:, cols], ALU.add)
+
+        def finish(i, pieces):
             back = bank(f"back{i}", i)
             for j in range(TILES):
                 nc.tensor.transpose(back[:, blk(j)], th[i][:, blk(j)], ident[:])
-            for cols in pieces:
-                nc.vector.tensor_tensor(asum[i][:, cols], a_sb[i][:, cols], ga[i][:, cols], ALU.add)
             for cols in pieces:
                 nc.vector.scalar_tensor_tensor(res[i][:, cols], back[:, cols], 1.0, asum[i][:, cols], ALU.add, ALU.mult)
                 nc.sync.dma_start(out[blk(i), cols], res[i][:, cols])
@@ -276,19 +278,24 @@ def tile_picked_cdswtriebfill_none_p_kernel(
         last = [half(0), blk(2), blk(3)]
         for i in range(TILES):
             a_product(i)
-        b_fetch_half(2, 1, False, sb("gb2b", [P, W], F32, "pa3")[:])
+        b_fetch(2, False, "pa3")
         b_fetch(3, False, "z_bf")
         a_copy(0, True)
         a_copy(1, False)
-        a_fetch(0, halves)
         a_copy(2, False)
-        a_fetch(1, halves)
-        b_gate(2)
         a_copy(3, False)
-        finish(0, whole)
+        a_fetch(0, halves)
+        b_gate(1, "z_q")
+        a_fetch(1, halves)
         a_fetch(2, halves)
+        a_sum(0, whole)
+        a_sum(1, whole)
+        finish(0, whole)
+        b_gate(2)
         b_gate(3)
-        finish(1, whole)
         a_fetch(3, last)
+        a_sum(2, whole)
+        finish(1, whole)
         finish(2, whole)
-        finish(3, last, "asum2")
+        a_sum(3, last)
+        finish(3, last)

@@ -147,9 +147,9 @@ def tile_picked_cdswtriebfill_none_p_kernel(
         th = {}
         wb_s = sb("wb_s", [P, S], U8)
 
-        def b_product(i, on_scalar, tag=None):
+        def b_product(i, on_scalar, tag=None, b=None):
             b_sb[i] = sb(f"b_sb{i}", [P, S], F32, tag)
-            acc = bank(f"b_acc{i}", i)
+            acc = bank(f"b_acc{i}", i if b is None else b)
             mx(acc[:], xb[:, blk(i)], sbb[:, blk(i)], wb_q[:], wb_s[:])
             if on_scalar:
                 nc.scalar.copy(b_sb[i][:], acc[:])
@@ -171,7 +171,7 @@ def tile_picked_cdswtriebfill_none_p_kernel(
 
         def b_gate(i, tag=None):
             th[i] = sb(f"th{i}", [P, S], F32, tag)
-            sum_t = bank(f"sum_t{i}", 4 + i)
+            sum_t = bank(f"sum_t{i}", (4, 5, 6, 3)[i])
             for j in range(TILES):
                 nc.tensor.matmul(sum_t[:, blk(j)], b_sb[i][:, blk(j)], ident[:], is_transpose=True, start=True, stop=False)
                 nc.tensor.matmul(sum_t[:, blk(j)], gb[i, j // 2][:, blk(j % 2)], ident[:], is_transpose=True, start=False, stop=True)
@@ -218,8 +218,8 @@ def tile_picked_cdswtriebfill_none_p_kernel(
         z_round(3)
         b_fetch_half(1, 1, True, sb("gb1b", [P, W], F32)[:])
         b_product(2, True, "ds2")
-        b_product(3, True, "ds3")
         b_gate(0)
+        b_gate(1)
 
         z_bf = sb("z_bf", [P, S * PACK], BF16)
         z_q = sb("z_q", [P, S], U32)
@@ -234,8 +234,8 @@ def tile_picked_cdswtriebfill_none_p_kernel(
 
 
         a_sb = [sb(f"a_sb{i}", [P, S], F32) for i in range(TILES)]
-        ga = [sb(f"ga{i}", [P, S], F32) for i in range(TILES)]
-        asum = {}
+        ga = {}
+        asum = [sb(f"asum{i}", [P, S], F32) for i in range(TILES - 1)]
         res = [sb(f"res{i}", [P, S], F32) for i in range(TILES)]
 
         a_acc = {}
@@ -255,18 +255,19 @@ def tile_picked_cdswtriebfill_none_p_kernel(
                 else:
                     nc.vector.tensor_scalar(a_sb[i][:, cols], acc[:, cols], 0.03125, None, ALU.mult)
 
-        def a_fetch(i, pieces):
+        def a_fetch(i, span, pieces, tag=None):
+            fetched = sb(f"ga{i}_{span.start}", [P, span.stop - span.start], F32, tag)
             for cols in pieces:
+                ga[i, cols.start] = fetched[:, cols.start - span.start : cols.stop - span.start]
                 offsets = l_n3[:, cols.start // 16 : cols.stop // 16]
-                nc.scalar.activation(ga[i][:, cols], a_sb[i][:].indirect(offsets), ACT.Copy)
+                nc.scalar.activation(ga[i, cols.start], a_sb[i][:].indirect(offsets), ACT.Copy)
+            return fetched
 
-        def a_sum(i, pieces):
-            asum[i] = sb(f"asum{i}", [P, S], F32)
-            for cols in pieces:
-                nc.vector.tensor_tensor(asum[i][:, cols], a_sb[i][:, cols], ga[i][:, cols], ALU.add)
+        def a_sum(i, cols, fetched):
+            (nc.gpsimd if i < TILES - 1 else nc.vector).tensor_tensor(asum[i][:, cols], a_sb[i][:, cols], fetched, ALU.add)
 
         def finish(i, pieces):
-            back = bank(f"back{i}", i)
+            back = bank(f"back{i}", (0, 1, 2, 7)[i])
             for j in range(TILES):
                 nc.tensor.transpose(back[:, blk(j)], th[i][:, blk(j)], ident[:])
             for cols in pieces:
@@ -279,23 +280,23 @@ def tile_picked_cdswtriebfill_none_p_kernel(
         for i in range(TILES):
             a_product(i)
         b_fetch(2, False, "pa3")
-        b_fetch(3, False, "z_bf")
         a_copy(0, True)
         a_copy(1, False)
         a_copy(2, False)
         a_copy(3, False)
-        a_fetch(0, halves)
-        b_gate(1, "z_q")
-        a_fetch(1, halves)
-        a_fetch(2, halves)
-        a_sum(0, whole)
-        a_sum(1, whole)
-        finish(0, whole)
+        b_product(3, False, b=7)
+        b_fetch(3, False)
+        for i in range(TILES - 1):
+            a_sum(i, whole[0], a_fetch(i, whole[0], halves)[:])
         b_gate(2)
-        b_gate(3)
-        a_fetch(3, last)
-        a_sum(2, whole)
+        a_fetch(3, half(0), last[:1])
+        finish(0, whole)
         finish(1, whole)
+        b_gate(3)
+        a_fetch(3, half(1), last[1:], "gb3")
+        asum.append(sb("asum3", [P, S], F32, "asum1"))
+        a_sum(3, last[0], ga[3, last[0].start])
         finish(2, whole)
-        a_sum(3, last)
+        for cols in last[1:]:
+            a_sum(3, cols, ga[3, cols.start])
         finish(3, last)

from contextlib import ExitStack

import concourse.mybir as mybir
from concourse.masks import make_identity

F32 = mybir.dt.float32
BF16 = mybir.dt.bfloat16
I32 = mybir.dt.int32
U32 = mybir.dt.uint32
U16 = mybir.dt.uint16
U8 = mybir.dt.uint8
FP8X4 = mybir.dt.float8_e4m3fn_x4
ALU = mybir.AluOpType
ACT = mybir.ActivationFunctionType

P = 128
PACK = 4
T = 2048
S = 512
W = 256
TILES = 4
FLOPS = 3 * 2 * 512 * 512 * 512


def tile_picked_cdswtriebfill_none_p_kernel(
    tc, x_words, x_scales, w1, gs, wb, offs, n1, n2, cand, cb, n3, n4, out
):
    nc = tc.nc
    with ExitStack() as ctx:
        lists = ctx.enter_context(tc.tile_pool(name="lists", bufs=1))
        keep = ctx.enter_context(tc.tile_pool(name="keep", bufs=1))
        psum = ctx.enter_context(tc.psum_pool(name="psum", bufs=1))

        def load_list(name, src):
            tile = lists.tile(list(src.shape), U16, name=name)
            nc.sync.dma_start(tile[:], src)
            return tile

        def sb(name, shape, dtype, tag=None):
            return keep.tile(shape, dtype, name=name, tag=tag or name, align_bytes=64)

        xs = sb("xs", [P, T], U8)
        nc.gpsimd.memset(xs[:].bitcast(I32), 0)
        l_offs = load_list("l_offs", offs)
        l_cand = load_list("l_cand", cand)
        l_cb = load_list("l_cb", cb)
        for q in range(4):
            nc.sync.dma_start(xs[32 * q : 32 * q + 4, :].bitcast(I32), x_scales[0, 4 * q : 4 * q + 4, :].bitcast(I32))
        w1_raw = sb("w1_raw", [P, PACK, S], F32)
        nc.sync.dma_start(w1_raw[:], w1.rearrange("(p j) c -> p j c", j=PACK))
        xw = sb("xw", [P, T], I32)
        nc.sync.dma_start(xw[:], x_words[0].rearrange("p c r -> p (c r)").bitcast(I32))
        l_n1 = load_list("l_n1", n1)
        wb_raw = sb("wb_raw", [P, PACK, S], F32)
        nc.sync.dma_start(wb_raw[:], wb.rearrange("(p j) c -> p j c", j=PACK))
        l_n2 = load_list("l_n2", n2)
        gain = sb("gain", [P, PACK], F32)
        nc.sync.dma_start(gain[:], gs.rearrange("(p j) o -> p (j o)", j=PACK))
        l_n4 = load_list("l_n4", n4)
        l_n3 = load_list("l_n3", n3)

        ident = sb("ident", [P, P], F32)
        make_identity(nc, ident[:])

        def pick_scales(name, lst, tag=None):
            picked = sb(name, [P, S], U8, tag)
            nc.vector.tensor_copy(picked[:], xs[:].indirect(lst[:]))
            return picked

        def pick_words(name, lst, tag=None):
            picked = sb(name, [P, S], U32, tag)
            nc.vector.tensor_copy(picked[:], xw[:].bitcast(U32).indirect(lst[:]))
            return picked

        def mx(acc, lhs, lhs_s, rhs, rhs_s):
            nc.tensor.matmul_mx(out=acc, lhsT=lhs.bitcast(FP8X4), lhsT_scale=lhs_s, rhs=rhs.bitcast(FP8X4),
                                rhs_scale=rhs_s, start=True, stop=True)

        def bank(name, b):
            return psum.tile([P, S], F32, name=name, tag=f"bank{b}")

        def blk(i):
            return slice(i * P, (i + 1) * P)

        def half(h):
            return slice(h * W, (h + 1) * W)

        def half_list(lst, h):
            return lst[:, h * (W // 16) : (h + 1) * (W // 16)]

        sq = pick_scales("sq", l_offs)
        sc = pick_scales("sc", l_cand)
        sbb = pick_scales("sbb", l_cb)

        w1_cols = w1_raw[:].rearrange("p j (m t) -> p m j t", t=TILES)
        w1_bf = [sb(f"w1_bf{h}", [P, 2, P * PACK], BF16) for h in range(2)]
        for h in range(2):
            nc.scalar.copy(w1_bf[h][:].rearrange("p t (m j) -> p m j t", j=PACK), w1_cols[:, :, :, 2 * h : 2 * h + 2])
        w1_q, w1_s = {}, {}

        def w1_quantise(t, tag=None):
            w1_q[t] = sb(f"w1_q{t}", [P, P], U32, tag)
            w1_s[t] = sb(f"w1_s{t}", [P, P], U8)
            nc.vector.quantize_mx(out=w1_q[t][:].bitcast(FP8X4), scales=w1_s[t][:], in_=w1_bf[t // 2][:, t % 2, :])

        w1_quantise(0)
        w1_quantise(1)
        xq = sb("xq", [P, S], U32, "w1_bf0")
        for h in range(2):
            nc.vector.tensor_copy(xq[:, half(h)], xw[:].bitcast(U32).indirect(half_list(l_offs, h)))

        ds = [sb(f"ds{t}", [P, S], F32) for t in range(TILES)]
        pa = [sb(f"pa{t}", [P, W], F32) for t in range(TILES)]
        pb = {}
        ra = {}

        y_acc = {}

        def y_product(t):
            y_acc[t] = bank(f"y_acc{t}", t)
            for cols in ([half(0), half(1)] if t == 0 else [slice(0, S)]):
                mx(y_acc[t][:, cols], w1_q[t][:], w1_s[t][:], xq[:, cols], sq[:, cols])

        def y_copy(t):
            nc.scalar.copy(ds[t][:], y_acc[t][:])

        def y_first(t):
            nc.scalar.activation(pa[t][:], ds[t][:].indirect(l_n1[:]), ACT.Copy)

        def y_second(t):
            pb[t] = sb(f"pb{t}", [P, W], F32)
            nc.vector.tensor_copy(pb[t][:], ds[t][:].indirect(l_n2[:]))

        def y_larger(t, tag=None):
            ra[t] = sb(f"ra{t}", [P, W], F32, tag)
            nc.vector.tensor_tensor(ra[t][:], pa[t][:], pb[t][:], ALU.max)

        def y_put(t):
            nc.scalar.activation(ds[t][:].indirect(l_n1[:]), ra[t][:], ACT.Copy)

        def z_round(t):
            for cols in ([half(0), half(1)] if t == TILES - 1 else [slice(0, S)]):
                nc.vector.tensor_scalar(z_pairs[:, t // 2, cols, t % 2], ds[t][:, cols], gain[:, t : t + 1], None, ALU.mult)

        b_sb = {}
        gb = {}
        th = {}
        wb_s = sb("wb_s", [P, S], U8)

        def b_product(i, on_scalar, tag=None, b=None):
            b_sb[i] = sb(f"b_sb{i}", [P, S], F32, tag)
            acc = bank(f"b_acc{i}", i if b is None else b)
            mx(acc[:], xb[:, blk(i)], sbb[:, blk(i)], wb_q[:], wb_s[:])
            if on_scalar:
                nc.scalar.copy(b_sb[i][:], acc[:])
            else:
                nc.vector.tensor_copy(b_sb[i][:], acc[:])

        def b_fetch_half(i, h, on_scalar, dst):
            gb[i, h] = dst
            window = b_sb[i][:].indirect(half_list(l_n4, h))
            if on_scalar:
                nc.scalar.activation(dst, window, ACT.Copy)
            else:
                nc.vector.tensor_copy(dst, window)

        def b_fetch(i, on_scalar, tag=None):
            fetched = sb(f"gb{i}", [P, S], F32, tag)
            for h in range(2):
                b_fetch_half(i, h, on_scalar, fetched[:, half(h)])

        def b_gate(i, tag=None):
            th[i] = sb(f"th{i}", [P, S], F32, tag)
            sum_t = bank(f"sum_t{i}", (4, 5, 6, 3)[i])
            for j in range(TILES):
                nc.tensor.matmul(sum_t[:, blk(j)], b_sb[i][:, blk(j)], ident[:], is_transpose=True, start=True, stop=False)
                nc.tensor.matmul(sum_t[:, blk(j)], gb[i, j // 2][:, blk(j % 2)], ident[:], is_transpose=True, start=False, stop=True)
            nc.scalar.activation(th[i][:], sum_t[:], ACT.Tanh, scale=0.5)

        xc = pick_words("xc", l_cand, "w1_raw")
        y_product(0)
        y_product(1)
        w1_quantise(2, "w1_q0")
        w1_quantise(3, "w1_s0")
        y_product(2)
        y_product(3)
        for t in (0, 2):
            y_copy(t)
            y_copy(t + 1)
            y_first(t)
            y_first(t + 1)
        wb_bf = sb("wb_bf", [P, S * PACK], BF16)
        wb_q = sb("wb_q", [P, S], U32)
        nc.vector.tensor_copy(
            wb_bf[:].rearrange("p (c i j) -> p c j i", i=4, j=PACK),
            wb_raw[:].rearrange("p j (c i) -> p c j i", i=4),
        )
        y_second(0)
        y_second(1)
        nc.vector.quantize_mx(out=wb_q[:].bitcast(FP8X4), scales=wb_s[:], in_=wb_bf[:])
        y_larger(0)
        y_larger(1)
        xb = pick_words("xb", l_cb, "pa0")
        y_second(2)
        y_second(3)
        y_larger(2)
        y_larger(3)
        z_pairs = sb("z_pairs", [P, 2, S, 2], BF16, "pa3")
        for t in range(TILES):
            y_put(t)
        b_product(0, False)
        b_product(1, False)
        b_fetch(0, False)
        z_round(0)
        z_round(1)
        z_round(2)
        b_fetch_half(1, 0, False, sb("gb1a", [P, W], F32)[:])
        z_round(3)
        b_fetch_half(1, 1, True, sb("gb1b", [P, W], F32)[:])
        b_product(2, True, "ds2")
        b_gate(0)
        b_gate(1)

        z_bf = sb("z_bf", [P, S * PACK], BF16)
        z_q = sb("z_q", [P, S], U32)
        z_s = sb("z_s", [P, S], U8)
        z_words = z_bf[:].bitcast(I32).rearrange("p (c u) -> p c u", u=2)
        pair_words = z_pairs[:].rearrange("p u c e -> p (u c e)").bitcast(I32).rearrange("p (u c) -> p c u", u=2)
        for h in range(2):
            nc.vector.tensor_copy(z_words[:, half(h)], pair_words[:, half(h)])
        for h in range(2):
            nc.vector.quantize_mx(out=z_q[:, half(h)].bitcast(FP8X4), scales=z_s[:, half(h)],
                                  in_=z_bf[:, h * W * PACK : (h + 1) * W * PACK])


        a_sb = [sb(f"a_sb{i}", [P, S], F32) for i in range(TILES)]
        ga = {}
        asum = [sb(f"asum{i}", [P, S], F32) for i in range(TILES - 1)]
        res = [sb(f"res{i}", [P, S], F32) for i in range(TILES)]

        a_acc = {}

        def a_product(i):
            pieces = [(half(0), 2), (half(1), 6)] if i == 0 else [(slice(0, S), (6 + i) % 8)]
            a_acc[i] = []
            for cols, b in pieces:
                acc = bank(f"a_acc{i}_{b}", b)
                mx(acc[:, cols], xc[:, blk(i)], sc[:, blk(i)], z_q[:, cols], z_s[:, cols])
                a_acc[i].append((cols, acc))

        def a_copy(i, on_scalar):
            for cols, acc in a_acc[i]:
                if on_scalar:
                    nc.scalar.activation(a_sb[i][:, cols], acc[:, cols], ACT.Copy, scale=0.03125)
                else:
                    nc.vector.tensor_scalar(a_sb[i][:, cols], acc[:, cols], 0.03125, None, ALU.mult)

        def a_fetch(i, span, pieces, tag=None):
            fetched = sb(f"ga{i}_{span.start}", [P, span.stop - span.start], F32, tag)
            for cols in pieces:
                ga[i, cols.start] = fetched[:, cols.start - span.start : cols.stop - span.start]
                offsets = l_n3[:, cols.start // 16 : cols.stop // 16]
                nc.scalar.activation(ga[i, cols.start], a_sb[i][:].indirect(offsets), ACT.Copy)
            return fetched

        def a_sum(i, cols, fetched):
            (nc.gpsimd if i < TILES - 1 else nc.vector).tensor_tensor(asum[i][:, cols], a_sb[i][:, cols], fetched, ALU.add)

        def finish(i, pieces):
            back = bank(f"back{i}", (0, 1, 2, 7)[i])
            for j in range(TILES):
                nc.tensor.transpose(back[:, blk(j)], th[i][:, blk(j)], ident[:])
            for cols in pieces:
                nc.vector.scalar_tensor_tensor(res[i][:, cols], back[:, cols], 1.0, asum[i][:, cols], ALU.add, ALU.mult)
                nc.sync.dma_start(out[blk(i), cols], res[i][:, cols])

        whole = [slice(0, S)]
        halves = [half(0), half(1)]
        last = [half(0), blk(2), blk(3)]
        for i in range(TILES):
            a_product(i)
        b_fetch(2, False, "pa3")
        a_copy(0, True)
        a_copy(1, False)
        a_copy(2, False)
        a_copy(3, False)
        b_product(3, False, b=7)
        b_fetch(3, False)
        for i in range(TILES - 1):
            a_sum(i, whole[0], a_fetch(i, whole[0], halves)[:])
        b_gate(2)
        a_fetch(3, half(0), last[:1])
        finish(0, whole)
        finish(1, whole)
        b_gate(3)
        a_fetch(3, half(1), last[1:], "gb3")
        asum.append(sb("asum3", [P, S], F32, "asum1"))
        a_sum(3, last[0], ga[3, last[0].start])
        finish(2, whole)
        for cols in last[1:]:
            a_sum(3, cols, ga[3, cols.start])
        finish(3, last)
